import numpy as np
import ml_dtypes


def mxq(x, axis, fmt="e4m3"):
    dtype, down = {"e4m3": (ml_dtypes.float8_e4m3fn, 7), "e5m2": (ml_dtypes.float8_e5m2, 14)}[fmt]
    v = np.moveaxis(np.asarray(x, np.float32).astype(ml_dtypes.bfloat16).astype(np.float64), axis, -1)
    blocks = v.reshape(v.shape[:-1] + (-1, 32))
    amax = np.abs(blocks).max(-1, keepdims=True)
    byte = np.maximum(np.where(amax > 0, np.frexp(amax)[1] - 1 + 127, 0) - down, 1)
    scale = np.exp2(byte - 127.0)
    codes = (blocks / scale).astype(np.float32).astype(dtype).astype(np.float64)
    return np.moveaxis((codes * scale).reshape(v.shape), -1, axis)


WIDE = False


def mx_kscale(k):
    if not WIDE:
        return np.ones(k)
    levels = np.array([30, -30])
    if k % 512:
        return np.exp2(np.random.permutation(np.resize(levels, k // 32))).repeat(32)
    a = np.empty((k // 512, 16))
    for p in range(k // 512):
        a[p, :8] = np.random.permutation(np.resize(levels, 8))
        for g in range(8):
            far = levels[np.abs(levels - a[p, g]) >= 10]
            a[p, g + 8] = far[np.random.randint(len(far))]
    return np.exp2(a.ravel()).repeat(32)


BF16 = ml_dtypes.bfloat16


def bf(x):
    return np.asarray(x, np.float32).astype(BF16)


def f64(x):
    return np.asarray(x).astype(np.float64)


E2M1 = np.array([0.0, 0.5, 1.0, 1.5, 2.0, 3.0, 4.0, 6.0, -0.0, -0.5, -1.0, -1.5, -2.0, -3.0, -4.0, -6.0])


def pack_weight(w, fmt):
    k, n = w.shape
    w = f64(bf(w)).reshape(k // 32, 32, n)
    amax = np.abs(w).max(1)
    if fmt == "e4m3":
        byte = np.frexp(amax)[1] - 1 + 127 - 7
    else:
        mant, ex = np.frexp(amax / 6.0)
        byte = np.where(mant > 0.5, ex, ex - 1) + 127
    byte = np.clip(np.where(amax > 0, byte, 1), 1, 254)
    scaled = (w * np.exp2(127.0 - byte)[:, None, :]).reshape(k, n).astype(np.float32)
    by_word = np.ascontiguousarray(scaled.reshape(k // 512, 128, 4, n).transpose(0, 1, 3, 2))
    if fmt == "e4m3":
        words = by_word.astype(ml_dtypes.float8_e4m3fn).view(np.uint8)
    else:
        c = by_word.astype(ml_dtypes.float4_e2m1fn).view(np.uint8) & 0xF
        words = c[..., 0::2] | (c[..., 1::2] << 4)
    return np.ascontiguousarray(words), np.ascontiguousarray(byte.astype(np.uint8).reshape(k // 512, 16, n))


def unpack_weight(words, scales, fmt):
    g, p, n, _ = words.shape
    if fmt == "e4m3":
        vals = np.ascontiguousarray(words).view(ml_dtypes.float8_e4m3fn).astype(np.float64)
    else:
        nib = np.empty((g, p, n, 4), np.uint8)
        nib[..., 0::2] = words & 0xF
        nib[..., 1::2] = words >> 4
        vals = E2M1[nib]
    vals = vals * np.repeat(np.exp2(scales.astype(np.float64) - 127.0), 8, axis=1)[..., None]
    return vals.transpose(0, 1, 3, 2).reshape(g * 512, n)
def pack4(w):
    words, scales = pack_weight(w, "e2m1")
    return words.reshape(words.shape[0], 128, -1), scales


def unpack4(words, scales):
    return unpack_weight(words.reshape(words.shape[0], 128, -1, 2), scales, "e2m1")


T, N, C = 512, 2048, 1024


def setup_inputs():
    s = mx_kscale(N)
    t = mx_kscale(N)
    vinv = np.random.standard_normal((N, N)) / np.sqrt(N) / s[:, None] * t
    vinv_words, vinv_scales = pack4(vinv)
    return {"resid": bf(np.random.standard_normal((T, N)) * s),
            "vinv_words": vinv_words,
            "vinv_scales": vinv_scales,
            "recw": bf(1 + 0.1 * np.random.standard_normal(N)),
            "grm": bf(np.random.standard_normal((N, C)) / np.sqrt(N) / t[:, None]),
            "gvar": bf(1 + 0.1 * np.random.standard_normal(T)),
            "mean": bf(0.3 * np.random.standard_normal(T))}


def reference(resid, vinv_words, vinv_scales, recw, grm, gvar, mean):
    vinv = unpack4(vinv_words, vinv_scales)
    p = mxq(f64(resid), 1, "e4m3") @ vinv
    a = p * f64(recw)[None, :]
    u = mxq(a, 1, "e5m2") @ mxq(f64(grm), 0, "e4m3")
    return u * f64(gvar)[:, None] + f64(mean)[:, None]

@@ -1,0 +1,343 @@
+from contextlib import ExitStack
+
+import concourse.mybir as mybir
+from concourse.masks import make_identity
+
+T, N, C = 512, 2048, 1024
+FLOPS = 2 * T * N * N + 2 * T * N * C
+
+F32 = mybir.dt.float32
+BF16 = mybir.dt.bfloat16
+I32 = mybir.dt.int32
+U32 = mybir.dt.uint32
+U8 = mybir.dt.uint8
+E4M3 = mybir.dt.float8_e4m3fn_x4
+E5M2 = mybir.dt.float8_e5m2_x4
+E2M1 = mybir.dt.float4_e2m1fn_x4
+ACT = mybir.ActivationFunctionType
+ALU = mybir.AluOpType
+
+P = 128
+PACK = 4
+KP = P * PACK
+PASSES = N // KP
+TRAIT_TILES = T // P
+HALVES = C // KP
+
+
+def tile_gblup_breeding_values_s9_kernel(
+    tc, resid, vinv_words, vinv_scales, recw, grm, gvar, mean, out
+):
+    nc = tc.nc
+    with ExitStack() as ctx:
+        keep = ctx.enter_context(tc.tile_pool(name="keep", bufs=1))
+        work = ctx.enter_context(tc.tile_pool(name="work", bufs=2))
+        psum = ctx.enter_context(tc.psum_pool(name="psum", bufs=1))
+        ctx.enter_context(tc.manual_schedule())
+
+        def kept(name, shape, dtype):
+            return keep.tile(shape, dtype, name=name, align_bytes=64)
+
+        def bank(b):
+            return psum.tile([P, KP], F32, name="bank%d" % b)
+
+        resid_v = resid.rearrange("(p m) k -> p m k", m=TRAIT_TILES)
+        out_v = out.rearrange("(p m) c -> p m c", m=TRAIT_TILES)
+        words_v = vinv_words.bitcast(I32).rearrange("g p w -> p g w")
+        scales_v = vinv_scales.bitcast(I32).rearrange("g (Q r) w -> r Q g w", r=4)
+
+        ident = kept("ident", [P, P], F32)
+        recw_rows = kept("recw_rows", [P, KP], BF16)
+        recw_sorted = kept("recw_sorted", [P, PACK, P], F32)
+        recw_col = kept("recw_col", [P, PACK, PASSES], F32)
+        gvar_raw = kept("gvar_raw", [P, TRAIT_TILES], BF16)
+        mean_raw = kept("mean_raw", [P, TRAIT_TILES], BF16)
+        gvar_col = kept("gvar_col", [P, TRAIT_TILES], F32)
+        mean_col = kept("mean_col", [P, TRAIT_TILES], F32)
+
+        r_raw = {}
+        r_codes = [kept("r_codes%d" % g, [P, T], U32) for g in range(PASSES)]
+        r_scales = [kept("r_scales%d" % g, [P, T], U8) for g in range(PASSES)]
+        v_raw = [kept("v_raw%d" % j, [P, PASSES, 256], I32) for j in range(PASSES)]
+        v_codes = [kept("v_codes%d" % j, [P, PASSES * 1024], U8) for j in range(PASSES)]
+        s_raw = [kept("s_raw%d" % j, [P, PASSES, 128], I32) for j in range(PASSES)]
+        v_scales = [kept("v_scales%d" % j, [P, PASSES * KP], U8) for j in range(PASSES)]
+        g_raw = [kept("g_raw%d" % j, [P, PACK, C], BF16) for j in range(PASSES)]
+        g_codes = {}
+        g_scales = {}
+        for j in range(PASSES):
+            for h in range(HALVES):
+                g_codes[j, h] = kept("g_codes%d_%d" % (j, h), [P, KP], U32)
+                g_scales[j, h] = kept("g_scales%d_%d" % (j, h), [P, KP], U8)
+        a_codes = [kept("a_codes%d" % j, [P, T], U32) for j in range(PASSES)]
+        a_scales = [kept("a_scales%d" % j, [P, T], U8) for j in range(PASSES)]
+
+        def load_resid(g, mm):
+            r_raw[g, mm] = kept("r_raw%d_%d" % (g, mm), [P, 2, KP], BF16)
+            nc.sync.dma_start(
+                out=r_raw[g, mm][:], in_=resid_v[:, 2 * mm : 2 * mm + 2, g * KP : (g + 1) * KP]
+            )
+
+        def load_words(j):
+            nc.sync.dma_start(out=v_raw[j][:], in_=words_v[:, :, 256 * j : 256 * (j + 1)])
+
+        def load_scales(j):
+            for r in range(4):
+                nc.sync.dma_start(
+                    out=s_raw[j][r:P:32, :, :], in_=scales_v[r][:, :, 128 * j : 128 * (j + 1)]
+                )
+
+        def load_grm(j):
+            rows = grm[j * KP : (j + 1) * KP, :].rearrange("(q t r) c -> t q r c", t=PACK, r=8)
+            for t in range(PACK):
+                nc.sync.dma_start(out=g_raw[j][:, t, :], in_=rows[t])
+
+        def sort_words(j, passes):
+            dst = v_codes[j][:].bitcast(I32).rearrange("p (g t q w) -> p g t q w", g=PASSES, t=PACK, w=4)
+            src = v_raw[j][:].rearrange("p g (q t w) -> p g t q w", t=PACK, w=4)
+            nc.vector.tensor_copy(out=dst[:, passes], in_=src[:, passes])
+
+        def sort_scales(j):
+            dst = v_scales[j][:].bitcast(I32).rearrange("p (g t q w) -> p g t q w", g=PASSES, t=PACK, w=2)
+            src = s_raw[j][:].rearrange("p g (q t w) -> p g t q w", t=PACK, w=2)
+            nc.vector.tensor_copy(out=dst, in_=src)
+
+        r_grouped = {}
+
+        def turn_resid(g, mm):
+            xt = bank(4 + 2 * (g % 2) + mm)
+            xt_v = xt[:].rearrange("p (m u i) -> p m u i", m=2, u=2)
+            words = r_raw[g, mm][:].bitcast(F32)
+            for m in range(2):
+                for u in range(2):
+                    nc.tensor.transpose(xt_v[:, m, u, :], words[:, m, u:256:2], ident[:])
+            r_grouped[g, mm] = kept("r_grouped%d_%d" % (g, mm), [P, 2 * P * PACK], BF16)
+            nc.scalar.copy(
+                out=r_grouped[g, mm][:].bitcast(F32).rearrange("p (m i u) -> p m i u", m=2, u=2),
+                in_=xt_v.rearrange("p m u i -> p m i u"),
+            )
+
+        def quantize_resid(g, mm):
+            cols = slice(mm * 2 * P, (mm + 1) * 2 * P)
+            nc.vector.quantize_mx(
+                out=r_codes[g][:, cols].bitcast(E4M3), scales=r_scales[g][:, cols], in_=r_grouped[g, mm][:]
+            )
+
+        p_bank = {}
+
+        def first_pass(j, t, g):
+            if g == 0:
+                p_bank[j, t] = bank(4 * (j % 2) + t)
+            col = g * PACK + t
+            nc.tensor.matmul_mx(
+                out=p_bank[j, t][:],
+                lhsT=v_codes[j][:, col * 256 : (col + 1) * 256].bitcast(E2M1),
+                lhsT_scale=v_scales[j][:, col * P : (col + 1) * P],
+                rhs=r_codes[g][:].bitcast(E4M3),
+                rhs_scale=r_scales[g][:],
+                start=(g == 0),
+                stop=(g == PASSES - 1),
+            )
+
+        a_rows = {}
+        a_grouped = {}
+
+        def weigh(j, t):
+            if t == 0:
+                a_rows[j] = work.tile([P, PACK, T], BF16, name="a_rows", align_bytes=64)
+            nc.scalar.activation(
+                out=a_rows[j][:, t, :], in_=p_bank[j, t][:], func=ACT.Copy, scale=recw_col[:, t, j : j + 1]
+            )
+
+        def interleave(copy, dst, src):
+            copy(
+                out=dst.rearrange("p (c i t) -> p c t i", i=4, t=PACK),
+                in_=src.rearrange("p t (c i) -> p c t i", i=4),
+            )
+
+        def group_a(j):
+            a_grouped[j] = work.tile([P, T * PACK], BF16, name="a_grouped", align_bytes=64)
+            interleave(nc.vector.tensor_copy, a_grouped[j][:], a_rows[j][:])
+
+        def quantize_a(j):
+            nc.vector.quantize_mx(out=a_codes[j][:].bitcast(E5M2), scales=a_scales[j][:], in_=a_grouped[j][:])
+
+        g_grouped = {}
+
+        def group_grm_vector(j):
+            g_grouped[j, 0] = work.tile([P, KP * PACK], BF16, name="g_grouped0", align_bytes=64)
+            interleave(nc.vector.tensor_copy, g_grouped[j, 0][:], g_raw[j][:, :, 0:KP])
+
+        def group_grm_scalar(j, part):
+            if part == 0:
+                g_grouped[j, 1] = work.tile([P, KP * PACK], BF16, name="g_grouped1", align_bytes=64)
+            w = KP // 2
+            interleave(
+                nc.scalar.copy,
+                g_grouped[j, 1][:, part * w * PACK : (part + 1) * w * PACK],
+                g_raw[j][:, :, KP + part * w : KP + (part + 1) * w],
+            )
+
+        def quantize_grm(j, h):
+            nc.vector.quantize_mx(
+                out=g_codes[j, h][:].bitcast(E4M3), scales=g_scales[j, h][:], in_=g_grouped[j, h][:]
+            )
+
+        u_bank = {}
+
+        def second_pass(h, m, j):
+            if j == 0:
+                u_bank[h, m] = bank(4 * h + m)
+            cols = slice(m * P, (m + 1) * P)
+            nc.tensor.matmul_mx(
+                out=u_bank[h, m][:],
+                lhsT=a_codes[j][:, cols].bitcast(E5M2),
+                lhsT_scale=a_scales[j][:, cols],
+                rhs=g_codes[j, h][:].bitcast(E4M3),
+                rhs_scale=g_scales[j, h][:],
+                start=(j == 0),
+                stop=(j == PASSES - 1),
+            )
+
+        def finish(h, m, on_vector):
+            res = kept("res%d_%d" % (h, m), [P, KP], F32)
+            if on_vector:
+                nc.vector.tensor_scalar(
+                    out=res[:], in0=u_bank[h, m][:], scalar1=gvar_col[:, m : m + 1],
+                    scalar2=mean_col[:, m : m + 1], op0=ALU.mult, op1=ALU.add,
+                )
+            else:
+                nc.scalar.activation(
+                    out=res[:], in_=u_bank[h, m][:], func=ACT.Identity,
+                    scale=gvar_col[:, m : m + 1], bias=mean_col[:, m : m + 1],
+                )
+            nc.sync.dma_start(out=out_v[:, m, h * KP : (h + 1) * KP], in_=res[:])
+
+        nc.scalar.dma_start(out=recw_rows[0:PASSES, :], in_=recw.rearrange("(j n) -> j n", n=KP))
+        for j in range(PASSES):
+            nc.vector.memset(s_raw[j][:], 0)
+        make_identity(nc, ident[:])
+        nc.gpsimd.memset(recw_sorted[:], 0.0)
+        nc.scalar.activation(
+            out=recw_sorted[0:PASSES].rearrange("j t (q r) -> j t q r", r=8),
+            in_=recw_rows[0:PASSES, :].rearrange("j (q t r) -> j t q r", t=PACK, r=8),
+            func=ACT.Copy,
+        )
+
+        for g in range(2):
+            for mm in range(2):
+                load_resid(g, mm)
+        load_words(0)
+        load_scales(0)
+        for g in range(2, 4):
+            for mm in range(2):
+                load_resid(g, mm)
+        load_words(1)
+        load_scales(1)
+        load_grm(0)
+        load_words(2)
+        load_scales(2)
+        nc.sync.dma_start(out=gvar_raw[:], in_=gvar.rearrange("(p m) -> p m", m=TRAIT_TILES))
+        nc.sync.dma_start(out=mean_raw[:], in_=mean.rearrange("(p m) -> p m", m=TRAIT_TILES))
+        load_grm(1)
+        load_scales(3)
+        load_grm(2)
+        load_words(3)
+        load_grm(3)
+
+        for g in range(2):
+            for mm in range(2):
+                turn_resid(g, mm)
+        quantize_resid(0, 0)
+        quantize_resid(0, 1)
+        sort_words(0, slice(0, 2))
+        sort_scales(0)
+        quantize_resid(1, 0)
+        quantize_resid(1, 1)
+        sort_words(0, slice(2, 4))
+
+        recw_bank = bank(3)
+        for t in range(PACK):
+            nc.tensor.transpose(recw_bank[:, t * P : (t + 1) * P], recw_sorted[:, t, :], ident[:])
+        nc.scalar.copy(
+            out=recw_col[:], in_=recw_bank[:].rearrange("p (t j) -> p t j", t=PACK)[:, :, 0:PASSES]
+        )
+
+        for t in range(PACK):
+            first_pass(0, t, 0)
+        for g in range(2, 4):
+            for mm in range(2):
+                turn_resid(g, mm)
+                quantize_resid(g, mm)
+        for g in range(1, 4):
+            for t in range(PACK):
+                first_pass(0, t, g)
+
+        def first_group(j):
+            for t in range(PACK):
+                for g in range(PASSES):
+                    first_pass(j, t, g)
+
+        sort_words(1, slice(0, 4))
+        sort_scales(1)
+        first_group(1)
+        group_grm_vector(0)
+        group_grm_scalar(0, 0)
+        group_grm_scalar(0, 1)
+        for t in range(PACK):
+            weigh(0, t)
+        sort_words(2, slice(0, 4))
+        quantize_grm(0, 0)
+        sort_scales(2)
+        quantize_grm(0, 1)
+        first_group(2)
+        for t in range(PACK):
+            weigh(1, t)
+        group_grm_vector(1)
+        group_a(0)
+        quantize_grm(1, 0)
+        quantize_a(0)
+        sort_scales(3)
+        sort_words(3, slice(0, 4))
+        first_group(3)
+        group_grm_scalar(1, 0)
+        group_grm_scalar(1, 1)
+        for t in range(PACK):
+            weigh(2, t)
+        nc.vector.tensor_copy(out=gvar_col[:], in_=gvar_raw[:])
+        nc.vector.tensor_copy(out=mean_col[:], in_=mean_raw[:])
+        group_grm_vector(2)
+        group_a(1)
+        quantize_grm(2, 0)
+        quantize_a(1)
+        group_a(2)
+        quantize_grm(1, 1)
+        quantize_a(2)
+        weigh(3, 0)
+        group_grm_scalar(2, 0)
+        for t in range(1, PACK):
+            weigh(3, t)
+        group_grm_scalar(2, 1)
+        group_grm_vector(3)
+        group_a(3)
+        quantize_grm(3, 0)
+        quantize_a(3)
+        group_grm_scalar(3, 0)
+        group_grm_scalar(3, 1)
+        quantize_grm(2, 1)
+        quantize_grm(3, 1)
+
+        for j in range(3):
+            for m in range(TRAIT_TILES):
+                second_pass(0, m, j)
+        for m in range(TRAIT_TILES):
+            second_pass(1, m, 0)
+        for m in range(TRAIT_TILES):
+            second_pass(0, m, 3)
+            finish(0, m, m % 2 == 1)
+        for m in range(TRAIT_TILES):
+            second_pass(1, m, 1)
+        for m in range(TRAIT_TILES):
+            second_pass(1, m, 2)
+            second_pass(1, m, 3)
+            finish(1, m, m % 2 == 1)

@@ -23,6 +23,7 @@ KP = P * PACK
 PASSES = N // KP
 TRAIT_TILES = T // P
 HALVES = C // KP
+WARM_A, WARM_B, WARM_C = 3, 2, 1
 
 
 def tile_gblup_breeding_values_s9_kernel(
@@ -58,9 +59,10 @@ def tile_gblup_breeding_values_s9_kernel(
         r_raw = {}
         r_codes = [kept("r_codes%d" % g, [P, T], U32) for g in range(PASSES)]
         r_scales = [kept("r_scales%d" % g, [P, T], U8) for g in range(PASSES)]
-        v_raw = [kept("v_raw%d" % j, [P, PASSES, 256], I32) for j in range(PASSES)]
-        v_codes = [kept("v_codes%d" % j, [P, PASSES * 1024], U8) for j in range(PASSES)]
-        s_raw = [kept("s_raw%d" % j, [P, PASSES, 128], I32) for j in range(PASSES)]
+        v_raw = {}
+        v_codes = {}
+        s_raw = {}
+        s_tile = {}
         v_scales = [kept("v_scales%d" % j, [P, PASSES * KP], U8) for j in range(PASSES)]
         g_raw = [kept("g_raw%d" % j, [P, PACK, C], BF16) for j in range(PASSES)]
         g_codes = {}
@@ -72,19 +74,29 @@ def tile_gblup_breeding_values_s9_kernel(
         a_codes = [kept("a_codes%d" % j, [P, T], U32) for j in range(PASSES)]
         a_scales = [kept("a_scales%d" % j, [P, T], U8) for j in range(PASSES)]
 
-        def load_resid(g, mm):
-            r_raw[g, mm] = kept("r_raw%d_%d" % (g, mm), [P, 2, KP], BF16)
-            nc.sync.dma_start(
-                out=r_raw[g, mm][:], in_=resid_v[:, 2 * mm : 2 * mm + 2, g * KP : (g + 1) * KP]
-            )
+        def load_resid(g, lo, hi):
+            raw = kept("r_raw%d_%d" % (g, lo), [P, 2 * (hi - lo), KP], BF16)
+            nc.sync.dma_start(out=raw[:], in_=resid_v[:, 2 * lo : 2 * hi, g * KP : (g + 1) * KP])
+            for mm in range(lo, hi):
+                r_raw[g, mm] = raw[:, 2 * (mm - lo) : 2 * (mm - lo) + 2, :]
 
-        def load_words(j):
-            nc.sync.dma_start(out=v_raw[j][:], in_=words_v[:, :, 256 * j : 256 * (j + 1)])
+        def load_words(j, lo, hi):
+            raw = kept("v_raw%d_%d" % (j, lo), [P, 2 * (hi - lo), 256], I32)
+            nc.sync.dma_start(out=raw[:], in_=words_v[:, 2 * lo : 2 * hi, 256 * j : 256 * (j + 1)])
+            for gg in range(lo, hi):
+                v_raw[j, gg] = raw[:, 2 * (gg - lo) : 2 * (gg - lo) + 2, :]
 
-        def load_scales(j):
+        def clear_scales(lo, hi):
+            raw = kept("s_raw%d" % lo, [P, PASSES, 128 * (hi - lo)], I32)
+            nc.vector.memset(raw[:], 0)
+            s_tile[lo] = raw
+            for j in range(lo, hi):
+                s_raw[j] = raw[:, :, 128 * (j - lo) : 128 * (j - lo + 1)]
+
+        def load_scales(lo, hi):
             for r in range(4):
                 nc.sync.dma_start(
-                    out=s_raw[j][r:P:32, :, :], in_=scales_v[r][:, :, 128 * j : 128 * (j + 1)]
+                    out=s_tile[lo][r:P:32, :, :], in_=scales_v[r][:, :, 128 * lo : 128 * hi]
                 )
 
         def load_grm(j):
@@ -92,26 +104,34 @@ def tile_gblup_breeding_values_s9_kernel(
             for t in range(PACK):
                 nc.sync.dma_start(out=g_raw[j][:, t, :], in_=rows[t])
 
-        def sort_words(j, passes):
-            dst = v_codes[j][:].bitcast(I32).rearrange("p (g t q w) -> p g t q w", g=PASSES, t=PACK, w=4)
-            src = v_raw[j][:].rearrange("p g (q t w) -> p g t q w", t=PACK, w=4)
-            nc.vector.tensor_copy(out=dst[:, passes], in_=src[:, passes])
+        def sort_words(j, gg):
+            v_codes[j, gg] = kept("v_codes%d_%d" % (j, gg), [P, 2 * 1024], U8)
+            dst = v_codes[j, gg][:].bitcast(I32).rearrange("p (g t q w) -> p g t q w", g=2, t=PACK, w=4)
+            src = v_raw[j, gg].rearrange("p g (q t w) -> p g t q w", t=PACK, w=4)
+            nc.vector.tensor_copy(out=dst, in_=src)
 
         def sort_scales(j):
             dst = v_scales[j][:].bitcast(I32).rearrange("p (g t q w) -> p g t q w", g=PASSES, t=PACK, w=2)
-            src = s_raw[j][:].rearrange("p g (q t w) -> p g t q w", t=PACK, w=2)
+            src = s_raw[j].rearrange("p g (q t w) -> p g t q w", t=PACK, w=2)
             nc.vector.tensor_copy(out=dst, in_=src)
 
         r_grouped = {}
+        r_sorted = {}
+
+        def sort_resid(g, mm):
+            r_sorted[g, mm] = work.tile([P, 2, 2, P], F32, name="r_sorted", bufs=4, align_bytes=64)
+            nc.vector.tensor_copy(
+                out=r_sorted[g, mm][:],
+                in_=r_raw[g, mm].bitcast(F32).rearrange("p m (i u) -> p m u i", u=2),
+            )
 
         def turn_resid(g, mm):
             xt = bank(4 + 2 * (g % 2) + mm)
             xt_v = xt[:].rearrange("p (m u i) -> p m u i", m=2, u=2)
-            words = r_raw[g, mm][:].bitcast(F32)
             for m in range(2):
                 for u in range(2):
-                    nc.tensor.transpose(xt_v[:, m, u, :], words[:, m, u:256:2], ident[:])
-            r_grouped[g, mm] = kept("r_grouped%d_%d" % (g, mm), [P, 2 * P * PACK], BF16)
+                    nc.tensor.transpose(xt_v[:, m, u, :], r_sorted[g, mm][:, m, u, :], ident[:])
+            r_grouped[g, mm] = work.tile([P, 2 * P * PACK], BF16, name="r_grouped", bufs=4, align_bytes=64)
             nc.scalar.copy(
                 out=r_grouped[g, mm][:].bitcast(F32).rearrange("p (m i u) -> p m i u", m=2, u=2),
                 in_=xt_v.rearrange("p m u i -> p m i u"),
@@ -129,9 +149,10 @@ def tile_gblup_breeding_values_s9_kernel(
             if g == 0:
                 p_bank[j, t] = bank(4 * (j % 2) + t)
             col = g * PACK + t
+            vcol = (g % 2) * PACK + t
             nc.tensor.matmul_mx(
                 out=p_bank[j, t][:],
-                lhsT=v_codes[j][:, col * 256 : (col + 1) * 256].bitcast(E2M1),
+                lhsT=v_codes[j, g // 2][:, vcol * 256 : (vcol + 1) * 256].bitcast(E2M1),
                 lhsT_scale=v_scales[j][:, col * P : (col + 1) * P],
                 rhs=r_codes[g][:].bitcast(E4M3),
                 rhs_scale=r_scales[g][:],
@@ -155,22 +176,28 @@ def tile_gblup_breeding_values_s9_kernel(
                 in_=src.rearrange("p t (c i) -> p c t i", i=4),
             )
 
-        def group_a(j):
-            a_grouped[j] = work.tile([P, T * PACK], BF16, name="a_grouped", align_bytes=64)
-            interleave(nc.vector.tensor_copy, a_grouped[j][:], a_rows[j][:])
+        def group_a(j, lo=0, hi=T):
+            if lo == 0:
+                a_grouped[j] = work.tile([P, T * PACK], BF16, name="a_grouped", align_bytes=64)
+            interleave(nc.vector.tensor_copy, a_grouped[j][:, lo * PACK : hi * PACK], a_rows[j][:, :, lo:hi])
 
-        def quantize_a(j):
-            nc.vector.quantize_mx(out=a_codes[j][:].bitcast(E5M2), scales=a_scales[j][:], in_=a_grouped[j][:])
+        def quantize_a(j, lo=0, hi=T):
+            nc.vector.quantize_mx(
+                out=a_codes[j][:, lo:hi].bitcast(E5M2),
+                scales=a_scales[j][:, lo:hi],
+                in_=a_grouped[j][:, lo * PACK : hi * PACK],
+            )
 
         g_grouped = {}
 
-        def group_grm_vector(j):
-            g_grouped[j, 0] = work.tile([P, KP * PACK], BF16, name="g_grouped0", align_bytes=64)
-            interleave(nc.vector.tensor_copy, g_grouped[j, 0][:], g_raw[j][:, :, 0:KP])
+        def group_grm_vector(j, lo=0, hi=KP):
+            if lo == 0:
+                g_grouped[j, 0] = work.tile([P, KP * PACK], BF16, name="g_grouped0", align_bytes=64)
+            interleave(nc.vector.tensor_copy, g_grouped[j, 0][:, lo * PACK : hi * PACK], g_raw[j][:, :, lo:hi])
 
         def group_grm_scalar(j, part):
             if part == 0:
-                g_grouped[j, 1] = work.tile([P, KP * PACK], BF16, name="g_grouped1", align_bytes=64)
+                g_grouped[j, 1] = work.tile([P, KP * PACK], BF16, name="g_grouped1", bufs=4, align_bytes=64)
             w = KP // 2
             interleave(
                 nc.scalar.copy,
@@ -199,23 +226,58 @@ def tile_gblup_breeding_values_s9_kernel(
                 stop=(j == PASSES - 1),
             )
 
-        def finish(h, m, on_vector):
-            res = kept("res%d_%d" % (h, m), [P, KP], F32)
+        res = [kept("res%d" % h, [P, TRAIT_TILES, KP], F32) for h in range(HALVES)]
+
+        def finish(h, m, on_vector, lo=0, hi=KP):
             if on_vector:
                 nc.vector.tensor_scalar(
-                    out=res[:], in0=u_bank[h, m][:], scalar1=gvar_col[:, m : m + 1],
+                    out=res[h][:, m, lo:hi], in0=u_bank[h, m][:, lo:hi], scalar1=gvar_col[:, m : m + 1],
                     scalar2=mean_col[:, m : m + 1], op0=ALU.mult, op1=ALU.add,
                 )
             else:
                 nc.scalar.activation(
-                    out=res[:], in_=u_bank[h, m][:], func=ACT.Identity,
+                    out=res[h][:, m, lo:hi], in_=u_bank[h, m][:, lo:hi], func=ACT.Identity,
                     scale=gvar_col[:, m : m + 1], bias=mean_col[:, m : m + 1],
                 )
-            nc.sync.dma_start(out=out_v[:, m, h * KP : (h + 1) * KP], in_=res[:])
+
+        def store(h, m0, m1, lo=0, hi=KP):
+            nc.sync.dma_start(out=out_v[:, m0:m1, h * KP + lo : h * KP + hi], in_=res[h][:, m0:m1, lo:hi])
+
+        warm_zeros = kept("warm_zeros", [P, KP], BF16)
+        warm_lhs = kept("warm_lhs", [P, P], U32)
+        warm_lhs_scales = kept("warm_lhs_scales", [P, P], U8)
+        warm_rhs = kept("warm_rhs", [P, KP], U32)
+        warm_rhs_scales = kept("warm_rhs_scales", [P, KP], U8)
+
+        def warm(count):
+            sink = bank(0)
+            for i in range(count):
+                nc.tensor.matmul_mx(
+                    out=sink[:], lhsT=warm_lhs[:].bitcast(E5M2), lhsT_scale=warm_lhs_scales[:],
+                    rhs=warm_rhs[:].bitcast(E4M3), rhs_scale=warm_rhs_scales[:], start=True, stop=True,
+                )
+
+        def first_group(j):
+            for t in range(PACK):
+                for g in range(PASSES):
+                    first_pass(j, t, g)
+
+        def first_row(g):
+            for t in range(PACK):
+                first_pass(0, t, g)
 
         nc.scalar.dma_start(out=recw_rows[0:PASSES, :], in_=recw.rearrange("(j n) -> j n", n=KP))
-        for j in range(PASSES):
-            nc.vector.memset(s_raw[j][:], 0)
+        nc.vector.memset(warm_zeros[:], 0.0)
+        nc.vector.memset(warm_rhs[:, 64:], 0)
+        nc.vector.memset(warm_rhs_scales[:, 64:].bitcast(I32), 0)
+        nc.vector.quantize_mx(out=warm_lhs[:].bitcast(E5M2), scales=warm_lhs_scales[:], in_=warm_zeros[:])
+        nc.vector.quantize_mx(
+            out=warm_rhs[:, 0:64].bitcast(E4M3), scales=warm_rhs_scales[:, 0:64], in_=warm_zeros[:, 0:256]
+        )
+        clear_scales(0, 1)
+        clear_scales(1, 2)
+        clear_scales(2, 3)
+        clear_scales(3, 4)
         make_identity(nc, ident[:])
         nc.gpsimd.memset(recw_sorted[:], 0.0)
         nc.scalar.activation(
@@ -224,120 +286,148 @@ def tile_gblup_breeding_values_s9_kernel(
             func=ACT.Copy,
         )
 
-        for g in range(2):
-            for mm in range(2):
-                load_resid(g, mm)
-        load_words(0)
-        load_scales(0)
-        for g in range(2, 4):
-            for mm in range(2):
-                load_resid(g, mm)
-        load_words(1)
-        load_scales(1)
+        load_resid(0, 0, 1)
+        load_resid(0, 1, 2)
+        load_resid(1, 0, 1)
+        load_words(0, 0, 1)
+        load_scales(0, 1)
+        load_resid(1, 1, 2)
+        load_resid(2, 0, 2)
+        load_resid(3, 0, 2)
+        load_words(0, 1, 2)
+        load_words(1, 0, 1)
+        load_scales(1, 2)
         load_grm(0)
-        load_words(2)
-        load_scales(2)
+        load_words(1, 1, 2)
+        load_grm(1)
+        load_words(2, 0, 2)
+        load_scales(2, 3)
+        load_grm(2)
+        load_words(3, 0, 2)
+        load_scales(3, 4)
+        load_grm(3)
         nc.sync.dma_start(out=gvar_raw[:], in_=gvar.rearrange("(p m) -> p m", m=TRAIT_TILES))
         nc.sync.dma_start(out=mean_raw[:], in_=mean.rearrange("(p m) -> p m", m=TRAIT_TILES))
-        load_grm(1)
-        load_scales(3)
-        load_grm(2)
-        load_words(3)
-        load_grm(3)
 
-        for g in range(2):
-            for mm in range(2):
-                turn_resid(g, mm)
-        quantize_resid(0, 0)
-        quantize_resid(0, 1)
-        sort_words(0, slice(0, 2))
-        sort_scales(0)
-        quantize_resid(1, 0)
-        quantize_resid(1, 1)
-        sort_words(0, slice(2, 4))
-
+        warm(WARM_A)
+        sort_resid(0, 0)
+        sort_resid(0, 1)
+        turn_resid(0, 0)
+        turn_resid(0, 1)
+        warm(WARM_B)
+        sort_resid(1, 0)
+        turn_resid(1, 0)
         recw_bank = bank(3)
         for t in range(PACK):
             nc.tensor.transpose(recw_bank[:, t * P : (t + 1) * P], recw_sorted[:, t, :], ident[:])
         nc.scalar.copy(
             out=recw_col[:], in_=recw_bank[:].rearrange("p (t j) -> p t j", t=PACK)[:, :, 0:PASSES]
         )
-
-        for t in range(PACK):
-            first_pass(0, t, 0)
-        for g in range(2, 4):
-            for mm in range(2):
-                turn_resid(g, mm)
-                quantize_resid(g, mm)
-        for g in range(1, 4):
-            for t in range(PACK):
-                first_pass(0, t, g)
-
-        def first_group(j):
-            for t in range(PACK):
-                for g in range(PASSES):
-                    first_pass(j, t, g)
-
-        sort_words(1, slice(0, 4))
+        warm(WARM_C)
+        sort_words(0, 0)
+        quantize_resid(0, 0)
+        sort_scales(0)
+        quantize_resid(0, 1)
+        first_pass(0, 0, 0)
+        first_pass(0, 1, 0)
+        sort_resid(1, 1)
+        turn_resid(1, 1)
+        quantize_resid(1, 0)
+        sort_resid(2, 0)
+        sort_resid(2, 1)
+        turn_resid(2, 0)
+        first_pass(0, 2, 0)
+        first_pass(0, 3, 0)
+        turn_resid(2, 1)
+        sort_resid(3, 0)
+        sort_resid(3, 1)
+        quantize_resid(1, 1)
+        turn_resid(3, 0)
+        turn_resid(3, 1)
+        first_row(1)
+        sort_words(0, 1)
+        quantize_resid(2, 0)
+        quantize_resid(2, 1)
+        first_row(2)
+        sort_words(1, 0)
+        quantize_resid(3, 0)
         sort_scales(1)
+        quantize_resid(3, 1)
+        first_row(3)
+        group_grm_vector(0, 0, KP // 2)
+        sort_words(1, 1)
+        group_grm_vector(0, KP // 2, KP)
         first_group(1)
-        group_grm_vector(0)
         group_grm_scalar(0, 0)
         group_grm_scalar(0, 1)
         for t in range(PACK):
             weigh(0, t)
-        sort_words(2, slice(0, 4))
         quantize_grm(0, 0)
-        sort_scales(2)
         quantize_grm(0, 1)
+        group_grm_vector(1)
+        sort_words(2, 0)
+        sort_scales(2)
+        sort_words(2, 1)
         first_group(2)
         for t in range(PACK):
             weigh(1, t)
-        group_grm_vector(1)
         group_a(0)
         quantize_grm(1, 0)
         quantize_a(0)
+        group_grm_vector(2)
+        sort_words(3, 0)
         sort_scales(3)
-        sort_words(3, slice(0, 4))
+        sort_words(3, 1)
         first_group(3)
         group_grm_scalar(1, 0)
+        weigh(2, 0)
+        weigh(2, 1)
         group_grm_scalar(1, 1)
-        for t in range(PACK):
-            weigh(2, t)
-        nc.vector.tensor_copy(out=gvar_col[:], in_=gvar_raw[:])
-        nc.vector.tensor_copy(out=mean_col[:], in_=mean_raw[:])
-        group_grm_vector(2)
+        weigh(2, 2)
+        weigh(2, 3)
         group_a(1)
         quantize_grm(2, 0)
         quantize_a(1)
-        group_a(2)
-        quantize_grm(1, 1)
-        quantize_a(2)
-        weigh(3, 0)
         group_grm_scalar(2, 0)
-        for t in range(1, PACK):
+        for t in range(PACK):
             weigh(3, t)
-        group_grm_scalar(2, 1)
         group_grm_vector(3)
-        group_a(3)
+        group_a(2)
         quantize_grm(3, 0)
-        quantize_a(3)
+        quantize_a(2)
+        nc.vector.tensor_copy(out=gvar_col[:], in_=gvar_raw[:])
+        nc.vector.tensor_copy(out=mean_col[:], in_=mean_raw[:])
+        group_a(3, 0, T // 2)
+        group_a(3, T // 2, T)
+        quantize_a(3, 0, T // 2)
+        quantize_a(3, T // 2, T)
+        group_grm_scalar(2, 1)
         group_grm_scalar(3, 0)
         group_grm_scalar(3, 1)
-        quantize_grm(2, 1)
-        quantize_grm(3, 1)
+        for j in range(1, PASSES):
+            quantize_grm(j, 1)
 
-        for j in range(3):
+        for j in range(PASSES - 1):
             for m in range(TRAIT_TILES):
                 second_pass(0, m, j)
         for m in range(TRAIT_TILES):
             second_pass(1, m, 0)
         for m in range(TRAIT_TILES):
-            second_pass(0, m, 3)
-            finish(0, m, m % 2 == 1)
+            second_pass(0, m, PASSES - 1)
+        finish(0, 0, False)
+        finish(0, 1, False)
+        store(0, 0, 2)
+        finish(0, 2, True)
+        finish(0, 3, False)
+        store(0, 2, 4)
         for m in range(TRAIT_TILES):
             second_pass(1, m, 1)
         for m in range(TRAIT_TILES):
             second_pass(1, m, 2)
             second_pass(1, m, 3)
-            finish(1, m, m % 2 == 1)
+        for m in range(TRAIT_TILES - 1):
+            finish(1, m, m % 2 == 0)
+            store(1, m, m + 1)
+        for lo in (0, KP // 2):
+            finish(1, TRAIT_TILES - 1, False, lo, lo + KP // 2)
+            store(1, TRAIT_TILES - 1, TRAIT_TILES, lo, lo + KP // 2)

@@ -23,7 +23,6 @@ KP = P * PACK
 PASSES = N // KP
 TRAIT_TILES = T // P
 HALVES = C // KP
-WARM_A, WARM_B, WARM_C = 3, 2, 1
 
 
 def tile_gblup_breeding_values_s9_kernel(
@@ -62,47 +61,49 @@ def tile_gblup_breeding_values_s9_kernel(
         v_raw = {}
         v_codes = {}
         s_raw = {}
-        s_tile = {}
-        v_scales = [kept("v_scales%d" % j, [P, PASSES * KP], U8) for j in range(PASSES)]
-        g_raw = [kept("g_raw%d" % j, [P, PACK, C], BF16) for j in range(PASSES)]
+        v_scales = {}
+        g_raw = {}
         g_codes = {}
         g_scales = {}
+        a_codes = {}
+        a_scales = {}
         for j in range(PASSES):
-            for h in range(HALVES):
+            for h in range(2):
                 g_codes[j, h] = kept("g_codes%d_%d" % (j, h), [P, KP], U32)
                 g_scales[j, h] = kept("g_scales%d_%d" % (j, h), [P, KP], U8)
-        a_codes = [kept("a_codes%d" % j, [P, T], U32) for j in range(PASSES)]
-        a_scales = [kept("a_scales%d" % j, [P, T], U8) for j in range(PASSES)]
+                a_codes[j, h] = kept("a_codes%d_%d" % (j, h), [P, 2 * P], U32)
+                a_scales[j, h] = kept("a_scales%d_%d" % (j, h), [P, 2 * P], U8)
 
-        def load_resid(g, lo, hi):
-            raw = kept("r_raw%d_%d" % (g, lo), [P, 2 * (hi - lo), KP], BF16)
-            nc.sync.dma_start(out=raw[:], in_=resid_v[:, 2 * lo : 2 * hi, g * KP : (g + 1) * KP])
-            for mm in range(lo, hi):
-                r_raw[g, mm] = raw[:, 2 * (mm - lo) : 2 * (mm - lo) + 2, :]
+        def load_resid(m):
+            r_raw[m] = kept("r_raw%d" % m, [P, N], BF16)
+            nc.sync.dma_start(out=r_raw[m][:], in_=resid_v[:, m, :])
 
-        def load_words(j, lo, hi):
-            raw = kept("v_raw%d_%d" % (j, lo), [P, 2 * (hi - lo), 256], I32)
-            nc.sync.dma_start(out=raw[:], in_=words_v[:, 2 * lo : 2 * hi, 256 * j : 256 * (j + 1)])
-            for gg in range(lo, hi):
-                v_raw[j, gg] = raw[:, 2 * (gg - lo) : 2 * (gg - lo) + 2, :]
+        def load_words(j0, j1, g0, g1):
+            raw = kept("v_raw%d_%d" % (j0, g0), [P, g1 - g0, 256 * (j1 - j0)], I32)
+            nc.sync.dma_start(out=raw[:], in_=words_v[:, g0:g1, 256 * j0 : 256 * j1])
+            for j in range(j0, j1):
+                for gg in range(g0 // 2, g1 // 2):
+                    v_raw[j, gg] = raw[:, 2 * gg - g0 : 2 * gg - g0 + 2, 256 * (j - j0) : 256 * (j - j0 + 1)]
 
-        def clear_scales(lo, hi):
-            raw = kept("s_raw%d" % lo, [P, PASSES, 128 * (hi - lo)], I32)
-            nc.vector.memset(raw[:], 0)
-            s_tile[lo] = raw
-            for j in range(lo, hi):
-                s_raw[j] = raw[:, :, 128 * (j - lo) : 128 * (j - lo + 1)]
+        s_tile = {}
 
-        def load_scales(lo, hi):
+        def clear_scales(j0, j1):
+            s_tile[j0] = kept("s_raw%d" % j0, [P, PASSES, 128 * (j1 - j0)], I32)
+            nc.vector.memset(s_tile[j0][:], 0)
+            for j in range(j0, j1):
+                s_raw[j] = s_tile[j0][:, :, 128 * (j - j0) : 128 * (j - j0 + 1)]
+
+        def load_scales(j0, j1):
             for r in range(4):
-                nc.sync.dma_start(
-                    out=s_tile[lo][r:P:32, :, :], in_=scales_v[r][:, :, 128 * lo : 128 * hi]
-                )
+                nc.sync.dma_start(out=s_tile[j0][r:P:32, :, :], in_=scales_v[r][:, :, 128 * j0 : 128 * j1])
 
-        def load_grm(j):
+        def load_grm(j, h0=0, h1=HALVES):
+            raw = kept("g_raw%d_%d" % (j, h0), [P, PACK, KP * (h1 - h0)], BF16)
             rows = grm[j * KP : (j + 1) * KP, :].rearrange("(q t r) c -> t q r c", t=PACK, r=8)
             for t in range(PACK):
-                nc.sync.dma_start(out=g_raw[j][:, t, :], in_=rows[t])
+                nc.sync.dma_start(out=raw[:, t, :], in_=rows[t][:, :, KP * h0 : KP * h1])
+            for h in range(h0, h1):
+                g_raw[j, h] = raw[:, :, KP * (h - h0) : KP * (h - h0 + 1)]
 
         def sort_words(j, gg):
             v_codes[j, gg] = kept("v_codes%d_%d" % (j, gg), [P, 2 * 1024], U8)
@@ -111,61 +112,76 @@ def tile_gblup_breeding_values_s9_kernel(
             nc.vector.tensor_copy(out=dst, in_=src)
 
         def sort_scales(j):
+            v_scales[j] = kept("v_scales%d" % j, [P, PASSES * KP], U8)
             dst = v_scales[j][:].bitcast(I32).rearrange("p (g t q w) -> p g t q w", g=PASSES, t=PACK, w=2)
             src = s_raw[j].rearrange("p g (q t w) -> p g t q w", t=PACK, w=2)
             nc.vector.tensor_copy(out=dst, in_=src)
 
         r_grouped = {}
         r_sorted = {}
+        r_turned = {}
 
-        def sort_resid(g, mm):
-            r_sorted[g, mm] = work.tile([P, 2, 2, P], F32, name="r_sorted", bufs=4, align_bytes=64)
+        def sort_resid(m, gg):
+            r_sorted[m, gg] = work.tile([P, 2, 2, P], F32, name="r_sorted", bufs=4, align_bytes=64)
             nc.vector.tensor_copy(
-                out=r_sorted[g, mm][:],
-                in_=r_raw[g, mm].bitcast(F32).rearrange("p m (i u) -> p m u i", u=2),
+                out=r_sorted[m, gg][:],
+                in_=r_raw[m][:, gg * 2 * KP : (gg + 1) * 2 * KP].bitcast(F32).rearrange("p (g i u) -> p g u i", g=2, u=2),
             )
 
-        def turn_resid(g, mm):
-            xt = bank(4 + 2 * (g % 2) + mm)
-            xt_v = xt[:].rearrange("p (m u i) -> p m u i", m=2, u=2)
-            for m in range(2):
+        def turn_resid(m, gg, b):
+            r_turned[m, gg] = bank(b)[:].rearrange("p (g u i) -> p g u i", g=2, u=2)
+            for g in range(2):
                 for u in range(2):
-                    nc.tensor.transpose(xt_v[:, m, u, :], r_sorted[g, mm][:, m, u, :], ident[:])
-            r_grouped[g, mm] = work.tile([P, 2 * P * PACK], BF16, name="r_grouped", bufs=4, align_bytes=64)
+                    nc.tensor.transpose(r_turned[m, gg][:, g, u, :], r_sorted[m, gg][:, g, u, :], ident[:])
+
+        def group_resid(m, gg):
+            xt_v = r_turned[m, gg]
+            r_grouped[m, gg] = kept("r_grouped%d_%d" % (m, gg), [P, 2 * P * PACK], BF16)
             nc.scalar.copy(
-                out=r_grouped[g, mm][:].bitcast(F32).rearrange("p (m i u) -> p m i u", m=2, u=2),
-                in_=xt_v.rearrange("p m u i -> p m i u"),
+                out=r_grouped[m, gg][:].bitcast(F32).rearrange("p (g i u) -> p g i u", g=2, u=2),
+                in_=xt_v.rearrange("p g u i -> p g i u"),
             )
 
-        def quantize_resid(g, mm):
-            cols = slice(mm * 2 * P, (mm + 1) * 2 * P)
-            nc.vector.quantize_mx(
-                out=r_codes[g][:, cols].bitcast(E4M3), scales=r_scales[g][:, cols], in_=r_grouped[g, mm][:]
-            )
+        def quantize_resid(m, gg):
+            cols = slice(m * P, (m + 1) * P)
+            for g in range(2):
+                nc.vector.quantize_mx(
+                    out=r_codes[2 * gg + g][:, cols].bitcast(E4M3),
+                    scales=r_scales[2 * gg + g][:, cols],
+                    in_=r_grouped[m, gg][:, g * KP : (g + 1) * KP],
+                )
 
         p_bank = {}
 
         def first_pass(j, t, g):
             if g == 0:
                 p_bank[j, t] = bank(4 * (j % 2) + t)
-            col = g * PACK + t
             vcol = (g % 2) * PACK + t
+            scol = g * PACK + t
             nc.tensor.matmul_mx(
                 out=p_bank[j, t][:],
                 lhsT=v_codes[j, g // 2][:, vcol * 256 : (vcol + 1) * 256].bitcast(E2M1),
-                lhsT_scale=v_scales[j][:, col * P : (col + 1) * P],
+                lhsT_scale=v_scales[j][:, scol * P : (scol + 1) * P],
                 rhs=r_codes[g][:].bitcast(E4M3),
                 rhs_scale=r_scales[g][:],
                 start=(g == 0),
                 stop=(g == PASSES - 1),
             )
 
+        def first_tile(j, t):
+            for g in range(PASSES):
+                first_pass(j, t, g)
+
+        def first_row(j, g):
+            for t in range(PACK):
+                first_pass(j, t, g)
+
         a_rows = {}
         a_grouped = {}
 
         def weigh(j, t):
             if t == 0:
-                a_rows[j] = work.tile([P, PACK, T], BF16, name="a_rows", align_bytes=64)
+                a_rows[j] = work.tile([P, PACK, T], BF16, name="a_rows", bufs=3, align_bytes=64)
             nc.scalar.activation(
                 out=a_rows[j][:, t, :], in_=p_bank[j, t][:], func=ACT.Copy, scale=recw_col[:, t, j : j + 1]
             )
@@ -176,34 +192,32 @@ def tile_gblup_breeding_values_s9_kernel(
                 in_=src.rearrange("p t (c i) -> p c t i", i=4),
             )
 
-        def group_a(j, lo=0, hi=T):
-            if lo == 0:
-                a_grouped[j] = work.tile([P, T * PACK], BF16, name="a_grouped", align_bytes=64)
-            interleave(nc.vector.tensor_copy, a_grouped[j][:, lo * PACK : hi * PACK], a_rows[j][:, :, lo:hi])
+        def group_a(j, mm):
+            a_grouped[j, mm] = work.tile([P, 2 * P * PACK], BF16, name="a_grouped", bufs=4, align_bytes=64)
+            interleave(nc.vector.tensor_copy, a_grouped[j, mm][:], a_rows[j][:, :, mm * 2 * P : (mm + 1) * 2 * P])
 
-        def quantize_a(j, lo=0, hi=T):
+        def quantize_a(j, mm):
             nc.vector.quantize_mx(
-                out=a_codes[j][:, lo:hi].bitcast(E5M2),
-                scales=a_scales[j][:, lo:hi],
-                in_=a_grouped[j][:, lo * PACK : hi * PACK],
+                out=a_codes[j, mm][:].bitcast(E5M2), scales=a_scales[j, mm][:], in_=a_grouped[j, mm][:]
             )
 
         g_grouped = {}
 
-        def group_grm_vector(j, lo=0, hi=KP):
-            if lo == 0:
-                g_grouped[j, 0] = work.tile([P, KP * PACK], BF16, name="g_grouped0", align_bytes=64)
-            interleave(nc.vector.tensor_copy, g_grouped[j, 0][:, lo * PACK : hi * PACK], g_raw[j][:, :, lo:hi])
-
-        def group_grm_scalar(j, part):
-            if part == 0:
-                g_grouped[j, 1] = work.tile([P, KP * PACK], BF16, name="g_grouped1", bufs=4, align_bytes=64)
+        def group_grm(copy, j, h, part):
+            if (j, h) not in g_grouped:
+                g_grouped[j, h] = work.tile([P, KP * PACK], BF16, name="g_grouped", bufs=6, align_bytes=64)
             w = KP // 2
             interleave(
-                nc.scalar.copy,
-                g_grouped[j, 1][:, part * w * PACK : (part + 1) * w * PACK],
-                g_raw[j][:, :, KP + part * w : KP + (part + 1) * w],
+                copy,
+                g_grouped[j, h][:, part * w * PACK : (part + 1) * w * PACK],
+                g_raw[j, h][:, :, part * w : (part + 1) * w],
             )
+
+        def gv(j, h, part):
+            group_grm(nc.vector.tensor_copy, j, h, part)
+
+        def gs(j, h, part):
+            group_grm(nc.scalar.copy, j, h, part)
 
         def quantize_grm(j, h):
             nc.vector.quantize_mx(
@@ -215,219 +229,152 @@ def tile_gblup_breeding_values_s9_kernel(
         def second_pass(h, m, j):
             if j == 0:
                 u_bank[h, m] = bank(4 * h + m)
-            cols = slice(m * P, (m + 1) * P)
+            cols = slice((m % 2) * P, (m % 2 + 1) * P)
             nc.tensor.matmul_mx(
                 out=u_bank[h, m][:],
-                lhsT=a_codes[j][:, cols].bitcast(E5M2),
-                lhsT_scale=a_scales[j][:, cols],
+                lhsT=a_codes[j, m // 2][:, cols].bitcast(E5M2),
+                lhsT_scale=a_scales[j, m // 2][:, cols],
                 rhs=g_codes[j, h][:].bitcast(E4M3),
                 rhs_scale=g_scales[j, h][:],
                 start=(j == 0),
                 stop=(j == PASSES - 1),
             )
 
-        res = [kept("res%d" % h, [P, TRAIT_TILES, KP], F32) for h in range(HALVES)]
-
         def finish(h, m, on_vector, lo=0, hi=KP):
+            res = kept("res%d_%d_%d" % (h, m, lo), [P, hi - lo], F32)
             if on_vector:
                 nc.vector.tensor_scalar(
-                    out=res[h][:, m, lo:hi], in0=u_bank[h, m][:, lo:hi], scalar1=gvar_col[:, m : m + 1],
+                    out=res[:], in0=u_bank[h, m][:, lo:hi], scalar1=gvar_col[:, m : m + 1],
                     scalar2=mean_col[:, m : m + 1], op0=ALU.mult, op1=ALU.add,
                 )
             else:
                 nc.scalar.activation(
-                    out=res[h][:, m, lo:hi], in_=u_bank[h, m][:, lo:hi], func=ACT.Identity,
+                    out=res[:], in_=u_bank[h, m][:, lo:hi], func=ACT.Identity,
                     scale=gvar_col[:, m : m + 1], bias=mean_col[:, m : m + 1],
                 )
+            nc.sync.dma_start(out=out_v[:, m, h * KP + lo : h * KP + hi], in_=res[:])
 
-        def store(h, m0, m1, lo=0, hi=KP):
-            nc.sync.dma_start(out=out_v[:, m0:m1, h * KP + lo : h * KP + hi], in_=res[h][:, m0:m1, lo:hi])
-
-        warm_zeros = kept("warm_zeros", [P, KP], BF16)
-        warm_lhs = kept("warm_lhs", [P, P], U32)
-        warm_lhs_scales = kept("warm_lhs_scales", [P, P], U8)
-        warm_rhs = kept("warm_rhs", [P, KP], U32)
-        warm_rhs_scales = kept("warm_rhs_scales", [P, KP], U8)
-
-        def warm(count):
-            sink = bank(0)
-            for i in range(count):
-                nc.tensor.matmul_mx(
-                    out=sink[:], lhsT=warm_lhs[:].bitcast(E5M2), lhsT_scale=warm_lhs_scales[:],
-                    rhs=warm_rhs[:].bitcast(E4M3), rhs_scale=warm_rhs_scales[:], start=True, stop=True,
-                )
-
-        def first_group(j):
+        def turn_recw(b):
+            recw_bank = bank(b)
             for t in range(PACK):
-                for g in range(PASSES):
-                    first_pass(j, t, g)
+                nc.tensor.transpose(recw_bank[:, t * P : (t + 1) * P], recw_sorted[:, t, :], ident[:])
+            nc.scalar.copy(
+                out=recw_col[:], in_=recw_bank[:].rearrange("p (t j) -> p t j", t=PACK)[:, :, 0:PASSES]
+            )
 
-        def first_row(g):
-            for t in range(PACK):
-                first_pass(0, t, g)
-
-        nc.scalar.dma_start(out=recw_rows[0:PASSES, :], in_=recw.rearrange("(j n) -> j n", n=KP))
-        nc.vector.memset(warm_zeros[:], 0.0)
-        nc.vector.memset(warm_rhs[:, 64:], 0)
-        nc.vector.memset(warm_rhs_scales[:, 64:].bitcast(I32), 0)
-        nc.vector.quantize_mx(out=warm_lhs[:].bitcast(E5M2), scales=warm_lhs_scales[:], in_=warm_zeros[:])
-        nc.vector.quantize_mx(
-            out=warm_rhs[:, 0:64].bitcast(E4M3), scales=warm_rhs_scales[:, 0:64], in_=warm_zeros[:, 0:256]
-        )
+        nc.sync.dma_start(out=recw_rows[0:PASSES, :], in_=recw.rearrange("(j n) -> j n", n=KP))
         clear_scales(0, 1)
         clear_scales(1, 2)
-        clear_scales(2, 3)
-        clear_scales(3, 4)
+        clear_scales(2, 4)
         make_identity(nc, ident[:])
         nc.gpsimd.memset(recw_sorted[:], 0.0)
-        nc.scalar.activation(
+        nc.vector.tensor_copy(
             out=recw_sorted[0:PASSES].rearrange("j t (q r) -> j t q r", r=8),
             in_=recw_rows[0:PASSES, :].rearrange("j (q t r) -> j t q r", t=PACK, r=8),
-            func=ACT.Copy,
         )
 
-        load_resid(0, 0, 1)
-        load_resid(0, 1, 2)
-        load_resid(1, 0, 1)
-        load_words(0, 0, 1)
+        for m in range(TRAIT_TILES):
+            load_resid(m)
+        load_words(0, 1, 0, 2)
         load_scales(0, 1)
-        load_resid(1, 1, 2)
-        load_resid(2, 0, 2)
-        load_resid(3, 0, 2)
-        load_words(0, 1, 2)
-        load_words(1, 0, 1)
+        load_words(0, 1, 2, 4)
+        load_grm(0, 0, 1)
+        load_words(1, 2, 0, 4)
         load_scales(1, 2)
-        load_grm(0)
-        load_words(1, 1, 2)
+        load_grm(0, 1, 2)
+        load_words(2, 3, 0, 4)
+        load_scales(2, 4)
         load_grm(1)
-        load_words(2, 0, 2)
-        load_scales(2, 3)
+        load_words(3, 4, 0, 4)
         load_grm(2)
-        load_words(3, 0, 2)
-        load_scales(3, 4)
         load_grm(3)
         nc.sync.dma_start(out=gvar_raw[:], in_=gvar.rearrange("(p m) -> p m", m=TRAIT_TILES))
         nc.sync.dma_start(out=mean_raw[:], in_=mean.rearrange("(p m) -> p m", m=TRAIT_TILES))
 
-        warm(WARM_A)
-        sort_resid(0, 0)
-        sort_resid(0, 1)
-        turn_resid(0, 0)
-        turn_resid(0, 1)
-        warm(WARM_B)
-        sort_resid(1, 0)
-        turn_resid(1, 0)
-        recw_bank = bank(3)
-        for t in range(PACK):
-            nc.tensor.transpose(recw_bank[:, t * P : (t + 1) * P], recw_sorted[:, t, :], ident[:])
-        nc.scalar.copy(
-            out=recw_col[:], in_=recw_bank[:].rearrange("p (t j) -> p t j", t=PACK)[:, :, 0:PASSES]
-        )
-        warm(WARM_C)
+        turn_recw(7)
+        for m in range(2):
+            for gg in range(2):
+                sort_resid(m, gg)
+                turn_resid(m, gg, 4 * gg + m)
+                group_resid(m, gg)
+        for gg in range(2):
+            for m in range(2, 4):
+                sort_resid(m, gg)
+                turn_resid(m, gg, 4 * gg + m)
+                group_resid(m, gg)
+                if gg == 0:
+                    quantize_resid(m - 2, 0)
         sort_words(0, 0)
-        quantize_resid(0, 0)
-        sort_scales(0)
-        quantize_resid(0, 1)
-        first_pass(0, 0, 0)
-        first_pass(0, 1, 0)
-        sort_resid(1, 1)
-        turn_resid(1, 1)
-        quantize_resid(1, 0)
-        sort_resid(2, 0)
-        sort_resid(2, 1)
-        turn_resid(2, 0)
-        first_pass(0, 2, 0)
-        first_pass(0, 3, 0)
-        turn_resid(2, 1)
-        sort_resid(3, 0)
-        sort_resid(3, 1)
-        quantize_resid(1, 1)
-        turn_resid(3, 0)
-        turn_resid(3, 1)
-        first_row(1)
-        sort_words(0, 1)
         quantize_resid(2, 0)
-        quantize_resid(2, 1)
-        first_row(2)
-        sort_words(1, 0)
+        sort_scales(0)
         quantize_resid(3, 0)
-        sort_scales(1)
-        quantize_resid(3, 1)
-        first_row(3)
-        group_grm_vector(0, 0, KP // 2)
+        for m in range(TRAIT_TILES):
+            quantize_resid(m, 1)
+        sort_words(0, 1)
+        for g in range(PASSES):
+            first_row(0, g)
+
+        gv(0, 0, 0)
+        gs(0, 0, 1)
+        sort_words(1, 0)
         sort_words(1, 1)
-        group_grm_vector(0, KP // 2, KP)
-        first_group(1)
-        group_grm_scalar(0, 0)
-        group_grm_scalar(0, 1)
+        sort_scales(1)
+        quantize_grm(0, 0)
         for t in range(PACK):
             weigh(0, t)
-        quantize_grm(0, 0)
-        quantize_grm(0, 1)
-        group_grm_vector(1)
+            first_tile(1, t)
+        gv(0, 1, 0)
+        gv(0, 1, 1)
         sort_words(2, 0)
-        sort_scales(2)
+        quantize_grm(0, 1)
         sort_words(2, 1)
-        first_group(2)
+        group_a(0, 0)
+        group_a(0, 1)
+        sort_scales(2)
+        quantize_a(0, 0)
+        sort_scales(3)
+        quantize_a(0, 1)
         for t in range(PACK):
             weigh(1, t)
-        group_a(0)
-        quantize_grm(1, 0)
-        quantize_a(0)
-        group_grm_vector(2)
-        sort_words(3, 0)
-        sort_scales(3)
-        sort_words(3, 1)
-        first_group(3)
-        group_grm_scalar(1, 0)
-        weigh(2, 0)
-        weigh(2, 1)
-        group_grm_scalar(1, 1)
-        weigh(2, 2)
-        weigh(2, 3)
-        group_a(1)
-        quantize_grm(2, 0)
-        quantize_a(1)
-        group_grm_scalar(2, 0)
-        for t in range(PACK):
-            weigh(3, t)
-        group_grm_vector(3)
-        group_a(2)
+        for j in (2, 3):
+            for t in range(PACK):
+                first_tile(j, t)
+                if t == 0:
+                    gs(j - 1, 1, 0)
+                weigh(j, t)
+            gs(j - 1, 1, 1)
+            group_a(j - 1, 0)
+            group_a(j - 1, 1)
+            gv(j - 1, 0, 0)
+            quantize_a(j - 1, 0)
+            if j == 2:
+                sort_words(3, 0)
+                sort_words(3, 1)
+            gv(j - 1, 0, 1)
+            quantize_a(j - 1, 1)
+            quantize_grm(j - 1, 0)
+        gv(3, 0, 0)
+        gv(3, 0, 1)
+        group_a(3, 0)
         quantize_grm(3, 0)
-        quantize_a(2)
+        group_a(3, 1)
+        quantize_a(3, 0)
+        quantize_a(3, 1)
+        gs(3, 1, 0)
+        gs(3, 1, 1)
         nc.vector.tensor_copy(out=gvar_col[:], in_=gvar_raw[:])
         nc.vector.tensor_copy(out=mean_col[:], in_=mean_raw[:])
-        group_a(3, 0, T // 2)
-        group_a(3, T // 2, T)
-        quantize_a(3, 0, T // 2)
-        quantize_a(3, T // 2, T)
-        group_grm_scalar(2, 1)
-        group_grm_scalar(3, 0)
-        group_grm_scalar(3, 1)
         for j in range(1, PASSES):
             quantize_grm(j, 1)
-
-        for j in range(PASSES - 1):
+        for h, j in ((0, 0), (0, 1), (0, 2), (1, 0), (0, 3)):
             for m in range(TRAIT_TILES):
-                second_pass(0, m, j)
+                second_pass(h, m, j)
         for m in range(TRAIT_TILES):
-            second_pass(1, m, 0)
+            finish(0, m, m == 3)
         for m in range(TRAIT_TILES):
-            second_pass(0, m, PASSES - 1)
-        finish(0, 0, False)
-        finish(0, 1, False)
-        store(0, 0, 2)
-        finish(0, 2, True)
-        finish(0, 3, False)
-        store(0, 2, 4)
-        for m in range(TRAIT_TILES):
-            second_pass(1, m, 1)
-        for m in range(TRAIT_TILES):
-            second_pass(1, m, 2)
-            second_pass(1, m, 3)
+            for j in range(1, PASSES):
+                second_pass(1, m, j)
         for m in range(TRAIT_TILES - 1):
             finish(1, m, m % 2 == 0)
-            store(1, m, m + 1)
         for lo in (0, KP // 2):
             finish(1, TRAIT_TILES - 1, False, lo, lo + KP // 2)
-            store(1, TRAIT_TILES - 1, TRAIT_TILES, lo, lo + KP // 2)

from contextlib import ExitStack

import concourse.mybir as mybir
from concourse.masks import make_identity

T, N, C = 512, 2048, 1024
FLOPS = 2 * T * N * N + 2 * T * N * C

F32 = mybir.dt.float32
BF16 = mybir.dt.bfloat16
I32 = mybir.dt.int32
U32 = mybir.dt.uint32
U8 = mybir.dt.uint8
E4M3 = mybir.dt.float8_e4m3fn_x4
E5M2 = mybir.dt.float8_e5m2_x4
E2M1 = mybir.dt.float4_e2m1fn_x4
ACT = mybir.ActivationFunctionType
ALU = mybir.AluOpType

P = 128
PACK = 4
KP = P * PACK
PASSES = N // KP
TRAIT_TILES = T // P
HALVES = C // KP


def tile_gblup_breeding_values_s9_kernel(
    tc, resid, vinv_words, vinv_scales, recw, grm, gvar, mean, out
):
    nc = tc.nc
    with ExitStack() as ctx:
        keep = ctx.enter_context(tc.tile_pool(name="keep", bufs=1))
        work = ctx.enter_context(tc.tile_pool(name="work", bufs=2))
        psum = ctx.enter_context(tc.psum_pool(name="psum", bufs=1))
        ctx.enter_context(tc.manual_schedule())

        def kept(name, shape, dtype):
            return keep.tile(shape, dtype, name=name, align_bytes=64)

        def bank(b):
            return psum.tile([P, KP], F32, name="bank%d" % b)

        resid_v = resid.rearrange("(p m) k -> p m k", m=TRAIT_TILES)
        out_v = out.rearrange("(p m) c -> p m c", m=TRAIT_TILES)
        words_v = vinv_words.bitcast(I32).rearrange("g p w -> p g w")
        scales_v = vinv_scales.bitcast(I32).rearrange("g (Q r) w -> r Q g w", r=4)

        ident = kept("ident", [P, P], F32)
        recw_rows = kept("recw_rows", [P, KP], BF16)
        recw_sorted = kept("recw_sorted", [P, PACK, P], F32)
        recw_col = kept("recw_col", [P, PACK, PASSES], F32)
        gvar_raw = kept("gvar_raw", [P, TRAIT_TILES], BF16)
        mean_raw = kept("mean_raw", [P, TRAIT_TILES], BF16)
        gvar_col = kept("gvar_col", [P, TRAIT_TILES], F32)
        mean_col = kept("mean_col", [P, TRAIT_TILES], F32)

        r_raw = {}
        r_codes = [kept("r_codes%d" % g, [P, T], U32) for g in range(PASSES)]
        r_scales = [kept("r_scales%d" % g, [P, T], U8) for g in range(PASSES)]
        v_raw = {}
        v_codes = {}
        s_raw = {}
        v_scales = {}
        g_raw = {}
        g_codes = {}
        g_scales = {}
        a_codes = {}
        a_scales = {}
        for j in range(PASSES):
            for h in range(2):
                g_codes[j, h] = kept("g_codes%d_%d" % (j, h), [P, KP], U32)
                g_scales[j, h] = kept("g_scales%d_%d" % (j, h), [P, KP], U8)
                a_codes[j, h] = kept("a_codes%d_%d" % (j, h), [P, 2 * P], U32)
                a_scales[j, h] = kept("a_scales%d_%d" % (j, h), [P, 2 * P], U8)

        def load_resid(m):
            r_raw[m] = kept("r_raw%d" % m, [P, N], BF16)
            nc.sync.dma_start(out=r_raw[m][:], in_=resid_v[:, m, :])

        def load_words(j0, j1, g0, g1):
            raw = kept("v_raw%d_%d" % (j0, g0), [P, g1 - g0, 256 * (j1 - j0)], I32)
            nc.sync.dma_start(out=raw[:], in_=words_v[:, g0:g1, 256 * j0 : 256 * j1])
            for j in range(j0, j1):
                for gg in range(g0 // 2, g1 // 2):
                    v_raw[j, gg] = raw[:, 2 * gg - g0 : 2 * gg - g0 + 2, 256 * (j - j0) : 256 * (j - j0 + 1)]

        s_tile = {}

        def clear_scales(j0, j1):
            s_tile[j0] = kept("s_raw%d" % j0, [P, PASSES, 128 * (j1 - j0)], I32)
            nc.vector.memset(s_tile[j0][:], 0)
            for j in range(j0, j1):
                s_raw[j] = s_tile[j0][:, :, 128 * (j - j0) : 128 * (j - j0 + 1)]

        def load_scales(j0, j1):
            for r in range(4):
                nc.sync.dma_start(out=s_tile[j0][r:P:32, :, :], in_=scales_v[r][:, :, 128 * j0 : 128 * j1])

        def load_grm(j, h0=0, h1=HALVES):
            raw = kept("g_raw%d_%d" % (j, h0), [P, PACK, KP * (h1 - h0)], BF16)
            rows = grm[j * KP : (j + 1) * KP, :].rearrange("(q t r) c -> t q r c", t=PACK, r=8)
            for t in range(PACK):
                nc.sync.dma_start(out=raw[:, t, :], in_=rows[t][:, :, KP * h0 : KP * h1])
            for h in range(h0, h1):
                g_raw[j, h] = raw[:, :, KP * (h - h0) : KP * (h - h0 + 1)]

        def sort_words(j, gg):
            v_codes[j, gg] = kept("v_codes%d_%d" % (j, gg), [P, 2 * 1024], U8)
            dst = v_codes[j, gg][:].bitcast(I32).rearrange("p (g t q w) -> p g t q w", g=2, t=PACK, w=4)
            src = v_raw[j, gg].rearrange("p g (q t w) -> p g t q w", t=PACK, w=4)
            nc.vector.tensor_copy(out=dst, in_=src)

        def sort_scales(j):
            v_scales[j] = kept("v_scales%d" % j, [P, PASSES * KP], U8)
            dst = v_scales[j][:].bitcast(I32).rearrange("p (g t q w) -> p g t q w", g=PASSES, t=PACK, w=2)
            src = s_raw[j].rearrange("p g (q t w) -> p g t q w", t=PACK, w=2)
            nc.vector.tensor_copy(out=dst, in_=src)

        r_grouped = {}
        r_sorted = {}
        r_turned = {}

        def sort_resid(m, gg):
            r_sorted[m, gg] = work.tile([P, 2, 2, P], F32, name="r_sorted", bufs=4, align_bytes=64)
            nc.vector.tensor_copy(
                out=r_sorted[m, gg][:],
                in_=r_raw[m][:, gg * 2 * KP : (gg + 1) * 2 * KP].bitcast(F32).rearrange("p (g i u) -> p g u i", g=2, u=2),
            )

        def turn_resid(m, gg, b):
            r_turned[m, gg] = bank(b)[:].rearrange("p (g u i) -> p g u i", g=2, u=2)
            for g in range(2):
                for u in range(2):
                    nc.tensor.transpose(r_turned[m, gg][:, g, u, :], r_sorted[m, gg][:, g, u, :], ident[:])

        def group_resid(m, gg):
            xt_v = r_turned[m, gg]
            r_grouped[m, gg] = kept("r_grouped%d_%d" % (m, gg), [P, 2 * P * PACK], BF16)
            nc.scalar.copy(
                out=r_grouped[m, gg][:].bitcast(F32).rearrange("p (g i u) -> p g i u", g=2, u=2),
                in_=xt_v.rearrange("p g u i -> p g i u"),
            )

        def quantize_resid(m, gg):
            cols = slice(m * P, (m + 1) * P)
            for g in range(2):
                nc.vector.quantize_mx(
                    out=r_codes[2 * gg + g][:, cols].bitcast(E4M3),
                    scales=r_scales[2 * gg + g][:, cols],
                    in_=r_grouped[m, gg][:, g * KP : (g + 1) * KP],
                )

        p_bank = {}

        def first_pass(j, t, g):
            if g == 0:
                p_bank[j, t] = bank(4 * (j % 2) + t)
            vcol = (g % 2) * PACK + t
            scol = g * PACK + t
            nc.tensor.matmul_mx(
                out=p_bank[j, t][:],
                lhsT=v_codes[j, g // 2][:, vcol * 256 : (vcol + 1) * 256].bitcast(E2M1),
                lhsT_scale=v_scales[j][:, scol * P : (scol + 1) * P],
                rhs=r_codes[g][:].bitcast(E4M3),
                rhs_scale=r_scales[g][:],
                start=(g == 0),
                stop=(g == PASSES - 1),
            )

        def first_tile(j, t):
            for g in range(PASSES):
                first_pass(j, t, g)

        def first_row(j, g):
            for t in range(PACK):
                first_pass(j, t, g)

        a_rows = {}
        a_grouped = {}

        def weigh(j, t):
            if t == 0:
                a_rows[j] = work.tile([P, PACK, T], BF16, name="a_rows", bufs=3, align_bytes=64)
            nc.scalar.activation(
                out=a_rows[j][:, t, :], in_=p_bank[j, t][:], func=ACT.Copy, scale=recw_col[:, t, j : j + 1]
            )

        def interleave(copy, dst, src):
            copy(
                out=dst.rearrange("p (c i t) -> p c t i", i=4, t=PACK),
                in_=src.rearrange("p t (c i) -> p c t i", i=4),
            )

        def group_a(j, mm):
            a_grouped[j, mm] = work.tile([P, 2 * P * PACK], BF16, name="a_grouped", bufs=4, align_bytes=64)
            interleave(nc.vector.tensor_copy, a_grouped[j, mm][:], a_rows[j][:, :, mm * 2 * P : (mm + 1) * 2 * P])

        def quantize_a(j, mm):
            nc.vector.quantize_mx(
                out=a_codes[j, mm][:].bitcast(E5M2), scales=a_scales[j, mm][:], in_=a_grouped[j, mm][:]
            )

        g_grouped = {}

        def group_grm(copy, j, h, part):
            if (j, h) not in g_grouped:
                g_grouped[j, h] = work.tile([P, KP * PACK], BF16, name="g_grouped", bufs=6, align_bytes=64)
            w = KP // 2
            interleave(
                copy,
                g_grouped[j, h][:, part * w * PACK : (part + 1) * w * PACK],
                g_raw[j, h][:, :, part * w : (part + 1) * w],
            )

        def gv(j, h, part):
            group_grm(nc.vector.tensor_copy, j, h, part)

        def gs(j, h, part):
            group_grm(nc.scalar.copy, j, h, part)

        def quantize_grm(j, h):
            nc.vector.quantize_mx(
                out=g_codes[j, h][:].bitcast(E4M3), scales=g_scales[j, h][:], in_=g_grouped[j, h][:]
            )

        u_bank = {}

        def second_pass(h, m, j):
            if j == 0:
                u_bank[h, m] = bank(4 * h + m)
            cols = slice((m % 2) * P, (m % 2 + 1) * P)
            nc.tensor.matmul_mx(
                out=u_bank[h, m][:],
                lhsT=a_codes[j, m // 2][:, cols].bitcast(E5M2),
                lhsT_scale=a_scales[j, m // 2][:, cols],
                rhs=g_codes[j, h][:].bitcast(E4M3),
                rhs_scale=g_scales[j, h][:],
                start=(j == 0),
                stop=(j == PASSES - 1),
            )

        def finish(h, m, on_vector, lo=0, hi=KP):
            res = kept("res%d_%d_%d" % (h, m, lo), [P, hi - lo], F32)
            if on_vector:
                nc.vector.tensor_scalar(
                    out=res[:], in0=u_bank[h, m][:, lo:hi], scalar1=gvar_col[:, m : m + 1],
                    scalar2=mean_col[:, m : m + 1], op0=ALU.mult, op1=ALU.add,
                )
            else:
                nc.scalar.activation(
                    out=res[:], in_=u_bank[h, m][:, lo:hi], func=ACT.Identity,
                    scale=gvar_col[:, m : m + 1], bias=mean_col[:, m : m + 1],
                )
            nc.sync.dma_start(out=out_v[:, m, h * KP + lo : h * KP + hi], in_=res[:])

        def turn_recw(b):
            recw_bank = bank(b)
            for t in range(PACK):
                nc.tensor.transpose(recw_bank[:, t * P : (t + 1) * P], recw_sorted[:, t, :], ident[:])
            nc.scalar.copy(
                out=recw_col[:], in_=recw_bank[:].rearrange("p (t j) -> p t j", t=PACK)[:, :, 0:PASSES]
            )

        nc.sync.dma_start(out=recw_rows[0:PASSES, :], in_=recw.rearrange("(j n) -> j n", n=KP))
        clear_scales(0, 1)
        clear_scales(1, 2)
        clear_scales(2, 4)
        make_identity(nc, ident[:])
        nc.gpsimd.memset(recw_sorted[:], 0.0)
        nc.vector.tensor_copy(
            out=recw_sorted[0:PASSES].rearrange("j t (q r) -> j t q r", r=8),
            in_=recw_rows[0:PASSES, :].rearrange("j (q t r) -> j t q r", t=PACK, r=8),
        )

        for m in range(TRAIT_TILES):
            load_resid(m)
        load_words(0, 1, 0, 2)
        load_scales(0, 1)
        load_words(0, 1, 2, 4)
        load_grm(0, 0, 1)
        load_words(1, 2, 0, 4)
        load_scales(1, 2)
        load_grm(0, 1, 2)
        load_words(2, 3, 0, 4)
        load_scales(2, 4)
        load_grm(1)
        load_words(3, 4, 0, 4)
        load_grm(2)
        load_grm(3)
        nc.sync.dma_start(out=gvar_raw[:], in_=gvar.rearrange("(p m) -> p m", m=TRAIT_TILES))
        nc.sync.dma_start(out=mean_raw[:], in_=mean.rearrange("(p m) -> p m", m=TRAIT_TILES))

        turn_recw(7)
        for m in range(2):
            for gg in range(2):
                sort_resid(m, gg)
                turn_resid(m, gg, 4 * gg + m)
                group_resid(m, gg)
        for gg in range(2):
            for m in range(2, 4):
                sort_resid(m, gg)
                turn_resid(m, gg, 4 * gg + m)
                group_resid(m, gg)
                if gg == 0:
                    quantize_resid(m - 2, 0)
        sort_words(0, 0)
        quantize_resid(2, 0)
        sort_scales(0)
        quantize_resid(3, 0)
        for m in range(TRAIT_TILES):
            quantize_resid(m, 1)
        sort_words(0, 1)
        for g in range(PASSES):
            first_row(0, g)

        gv(0, 0, 0)
        gs(0, 0, 1)
        sort_words(1, 0)
        sort_words(1, 1)
        sort_scales(1)
        quantize_grm(0, 0)
        for t in range(PACK):
            weigh(0, t)
            first_tile(1, t)
        gv(0, 1, 0)
        gv(0, 1, 1)
        sort_words(2, 0)
        quantize_grm(0, 1)
        sort_words(2, 1)
        group_a(0, 0)
        group_a(0, 1)
        sort_scales(2)
        quantize_a(0, 0)
        sort_scales(3)
        quantize_a(0, 1)
        for t in range(PACK):
            weigh(1, t)
        for j in (2, 3):
            for t in range(PACK):
                first_tile(j, t)
                if t == 0:
                    gs(j - 1, 1, 0)
                weigh(j, t)
            gs(j - 1, 1, 1)
            group_a(j - 1, 0)
            group_a(j - 1, 1)
            gv(j - 1, 0, 0)
            quantize_a(j - 1, 0)
            if j == 2:
                sort_words(3, 0)
                sort_words(3, 1)
            gv(j - 1, 0, 1)
            quantize_a(j - 1, 1)
            quantize_grm(j - 1, 0)
        gv(3, 0, 0)
        gv(3, 0, 1)
        group_a(3, 0)
        quantize_grm(3, 0)
        group_a(3, 1)
        quantize_a(3, 0)
        quantize_a(3, 1)
        gs(3, 1, 0)
        gs(3, 1, 1)
        nc.vector.tensor_copy(out=gvar_col[:], in_=gvar_raw[:])
        nc.vector.tensor_copy(out=mean_col[:], in_=mean_raw[:])
        for j in range(1, PASSES):
            quantize_grm(j, 1)
        for h, j in ((0, 0), (0, 1), (0, 2), (1, 0), (0, 3)):
            for m in range(TRAIT_TILES):
                second_pass(h, m, j)
        for m in range(TRAIT_TILES):
            finish(0, m, m == 3)
        for m in range(TRAIT_TILES):
            for j in range(1, PASSES):
                second_pass(1, m, j)
        for m in range(TRAIT_TILES - 1):
            finish(1, m, m % 2 == 0)
        for lo in (0, KP // 2):
            finish(1, TRAIT_TILES - 1, False, lo, lo + KP // 2)
